import numpy as np
import ml_dtypes


def mxq(x, axis, fmt="e4m3"):
    dtype, down = {"e4m3": (ml_dtypes.float8_e4m3fn, 7), "e5m2": (ml_dtypes.float8_e5m2, 14)}[fmt]
    v = np.moveaxis(np.asarray(x, np.float32).astype(ml_dtypes.bfloat16).astype(np.float64), axis, -1)
    blocks = v.reshape(v.shape[:-1] + (-1, 32))
    amax = np.abs(blocks).max(-1, keepdims=True)
    byte = np.maximum(np.where(amax > 0, np.frexp(amax)[1] - 1 + 127, 0) - down, 1)
    scale = np.exp2(byte - 127.0)
    codes = (blocks / scale).astype(np.float32).astype(dtype).astype(np.float64)
    return np.moveaxis((codes * scale).reshape(v.shape), -1, axis)


WIDE = False


def mx_kscale(k):
    if not WIDE:
        return np.ones(k)
    levels = np.array([10, -10, 5, -5, 0])
    if k % 512:
        return np.exp2(np.random.permutation(np.resize(levels, k // 32))).repeat(32)
    a = np.empty((k // 512, 16))
    for p in range(k // 512):
        a[p, :8] = np.random.permutation(np.resize(levels, 8))
        for g in range(8):
            far = levels[np.abs(levels - a[p, g]) >= 10]
            a[p, g + 8] = far[np.random.randint(len(far))]
    return np.exp2(a.ravel()).repeat(32)


def f64(x):
    return np.asarray(x).astype(np.float64)


def striped(idx):
    return np.tile(np.asarray(idx).reshape(-1, 16).T, (8, 1)).astype(np.uint16)


def unstriped(offs):
    return offs[:16].T.reshape(-1).astype(np.int64)


E2M1 = np.array([0.0, 0.5, 1.0, 1.5, 2.0, 3.0, 4.0, 6.0, -0.0, -0.5, -1.0, -1.5, -2.0, -3.0, -4.0, -6.0])


def pack_weight(w, fmt):
    k, n = w.shape
    w = f64(np.asarray(w, np.float32).astype(ml_dtypes.bfloat16)).reshape(k // 32, 32, n)
    amax = np.abs(w).max(1)
    if fmt == "e4m3":
        byte = np.frexp(amax)[1] - 1 + 127 - 7
    else:
        mant, ex = np.frexp(amax / 6.0)
        byte = np.where(mant > 0.5, ex, ex - 1) + 127
    byte = np.clip(np.where(amax > 0, byte, 1), 1, 254)
    scaled = (w * np.exp2(127.0 - byte)[:, None, :]).reshape(k, n).astype(np.float32)
    by_word = np.ascontiguousarray(scaled.reshape(k // 512, 128, 4, n).transpose(0, 1, 3, 2))
    if fmt == "e4m3":
        words = by_word.astype(ml_dtypes.float8_e4m3fn).view(np.uint8)
    else:
        c = by_word.astype(ml_dtypes.float4_e2m1fn).view(np.uint8) & 0xF
        words = (c[..., 0::2] | (c[..., 1::2] << 4)).reshape(k // 512, 128, 2 * n)
    return np.ascontiguousarray(words), np.ascontiguousarray(byte.astype(np.uint8).reshape(k // 512, 16, n))


def unpack_weight(words, scales, fmt):
    g, _, n = scales.shape
    words = np.ascontiguousarray(words).reshape(g, 128, n, -1)
    if fmt == "e4m3":
        vals = words.view(ml_dtypes.float8_e4m3fn).astype(np.float64)
    else:
        nib = np.empty((g, 128, n, 4), np.uint8)
        nib[..., 0::2] = words & 0xF
        nib[..., 1::2] = words >> 4
        vals = E2M1[nib]
    vals = vals * np.repeat(np.exp2(scales.astype(np.float64) - 127.0), 8, axis=1)[..., None]
    return vals.transpose(0, 1, 3, 2).reshape(g * 512, n)


K, R, F, T, J, G = 512, 128, 512, 2048, 512, 64


def setup_inputs():
    n = np.random.standard_normal
    idx = np.random.permutation(T)[:J]
    fk = mx_kscale(K)
    ff = mx_kscale(F)
    tabp = pack_weight(n((K, T)) / fk[:, None], "e4m3")
    return {
        "tab_words": tabp[0],
        "tab_scales": tabp[1],
        "w1": (n((K, R)) * 1 / np.sqrt(K) * fk[:, None]).astype(np.float32),
        "share": (np.random.uniform(0.3, 1.2, (R, 1))).astype(np.float32),
        "wo": (n((F, R)) * 1 / np.sqrt(F) * ff[:, None]).astype(np.float32),
        "dy": (n((F, G)) / ff[:, None]).astype(np.float32),
        "og": (np.random.uniform(0.3, 1.0, (R, 1))).astype(np.float32),
        "base": (0.3 * n((R, J))).astype(np.float32),
        "offs": striped(idx),
    }


def reference(tab_words, tab_scales, w1, share, wo, dy, og, base, offs):
    idx = unstriped(offs)
    tabu = unpack_weight(tab_words, tab_scales, "e4m3")
    w1q = mxq(f64(w1), 0, "e4m3")
    tabidxg = tabu[:, idx]
    a = w1q.T @ tabidxg
    m1 = a.reshape(R, G, J // G).mean(axis=2)
    v1 = np.sqrt(np.square(a).reshape(R, G, J // G).mean(axis=2) - np.square(m1) + 0.05)
    u1 = np.tanh(v1 + m1 * f64(share))
    woq = mxq(f64(wo), 0, "e4m3")
    dyq = mxq(f64(dy), 0, "e4m3")
    c0 = woq.T @ dyq
    dv1 = c0 * (1.0 - np.square(u1))
    e1 = dv1 * 0.5 / np.sqrt(np.square(a).reshape(R, G, J // G).mean(axis=2) - np.square(m1) + 0.05) / 8.0
    r1 = np.repeat(e1, J // G, axis=1)
    dm1 = c0 * (1.0 - np.square(u1)) * f64(share) + dv1 * 0.5 / np.sqrt(np.square(a).reshape(R, G, J // G).mean(axis=2) - np.square(m1) + 0.05) * (-1.0) * m1 * 2.0
    e2 = dm1 / 8.0
    r2 = np.repeat(e2, J // G, axis=1)
    da = r1 * a * 2.0 + r2
    hda = da * 2.0
    he2 = hda.reshape(R, G, J // G).sum(axis=2)
    hdm1 = he2 / 8.0
    e51 = hdm1 * 2.0 * m1 * (-1.0) * dv1 * 0.5 / np.square(np.sqrt(np.square(a).reshape(R, G, J // G).mean(axis=2) - np.square(m1) + 0.05)) * (-1.0) * 0.5 / np.sqrt(np.square(a).reshape(R, G, J // G).mean(axis=2) - np.square(m1) + 0.05) / 8.0
    r51 = np.repeat(e51, J // G, axis=1)
    hr1 = hda * 2.0 * a
    he1 = hr1.reshape(R, G, J // G).sum(axis=2)
    e52 = he1 / 8.0 * dv1 * 0.5 / np.square(np.sqrt(np.square(a).reshape(R, G, J // G).mean(axis=2) - np.square(m1) + 0.05)) * (-1.0) * 0.5 / np.sqrt(np.square(a).reshape(R, G, J // G).mean(axis=2) - np.square(m1) + 0.05) / 8.0
    r52 = np.repeat(e52, J // G, axis=1)
    hdv1 = hdm1 * 2.0 * m1 * (-1.0) / np.sqrt(np.square(a).reshape(R, G, J // G).mean(axis=2) - np.square(m1) + 0.05) * 0.5 + he1 / 8.0 / np.sqrt(np.square(a).reshape(R, G, J // G).mean(axis=2) - np.square(m1) + 0.05) * 0.5
    hu1 = hdm1 * f64(share) * c0 * (-1.0) * u1 * 2.0 + hdv1 * c0 * (-1.0) * u1 * 2.0
    hv1 = hu1 * (1.0 - np.square(u1))
    e53 = hv1 * 0.5 / np.sqrt(np.square(a).reshape(R, G, J // G).mean(axis=2) - np.square(m1) + 0.05) / 8.0
    r53 = np.repeat(e53, J // G, axis=1)
    hm1 = hdm1 * 2.0 * m1 * (-1.0) * dv1 * 0.5 / np.square(np.sqrt(np.square(a).reshape(R, G, J // G).mean(axis=2) - np.square(m1) + 0.05)) * (-1.0) * 0.5 / np.sqrt(np.square(a).reshape(R, G, J // G).mean(axis=2) - np.square(m1) + 0.05) * (-1.0) * m1 * 2.0 + hdm1 * 2.0 * dv1 * 0.5 / np.sqrt(np.square(a).reshape(R, G, J // G).mean(axis=2) - np.square(m1) + 0.05) * (-1.0) + he1 / 8.0 * dv1 * 0.5 / np.square(np.sqrt(np.square(a).reshape(R, G, J // G).mean(axis=2) - np.square(m1) + 0.05)) * (-1.0) * 0.5 / np.sqrt(np.square(a).reshape(R, G, J // G).mean(axis=2) - np.square(m1) + 0.05) * (-1.0) * m1 * 2.0 + hu1 * (1.0 - np.square(u1)) * f64(share) + hv1 * 0.5 / np.sqrt(np.square(a).reshape(R, G, J // G).mean(axis=2) - np.square(m1) + 0.05) * (-1.0) * m1 * 2.0
    e54 = hm1 / 8.0
    r54 = np.repeat(e54, J // G, axis=1)
    ha = hda * 2.0 * r1 + r51 * a * 2.0 + r52 * a * 2.0 + r53 * a * 2.0 + r54
    y = ha * f64(og) + f64(base)
    return y

@@ -1,0 +1,177 @@
+from contextlib import ExitStack
+
+import concourse.mybir as mybir
+
+K, R, F, T, J, G = 512, 128, 512, 2048, 512, 64
+FLOPS = 2 * K * R * J + 2 * F * R * G
+
+F32 = mybir.dt.float32
+BF16 = mybir.dt.bfloat16
+I32 = mybir.dt.int32
+U32 = mybir.dt.uint32
+U16 = mybir.dt.uint16
+U8 = mybir.dt.uint8
+FP8X4 = mybir.dt.float8_e4m3fn_x4
+ALU = mybir.AluOpType
+ACT = mybir.ActivationFunctionType
+AX = mybir.AxisListType
+
+P = 128
+PACK = 4
+POOL = J // G
+EPS = 0.05
+HALVES = 2
+JH = J // HALVES
+GH = G // HALVES
+
+
+def tile_attend_gpspreadpool_kernel(tc, tab_words, tab_scales, w1, share, wo, dy, og, base, offs, out):
+    nc = tc.nc
+    mult, add, sub = ALU.mult, ALU.add, ALU.subtract
+
+    with ExitStack() as ctx:
+        sb = ctx.enter_context(tc.tile_pool(name="sb", bufs=1))
+        psum = ctx.enter_context(tc.psum_pool(name="psum", bufs=1))
+
+        def small(name, cols=G):
+            return sb.tile([P, cols], F32, name=name)
+
+        def spread(ap, h):
+            return ap[:, h * GH : (h + 1) * GH].unsqueeze(2).to_broadcast([P, GH, POOL])
+
+        def grouped(ap):
+            return ap.rearrange("p (g i) -> p g i", i=POOL)
+
+        offsets = sb.tile([P, J // 16], U16, name="offsets")
+        scale_win = sb.tile([P, T], U8, name="scale_win")
+        word_win = sb.tile([P, T], I32, name="word_win")
+        w1_raw = sb.tile([P, PACK * R], F32, name="w1_raw", tag="stage")
+
+        nc.vector.memset(scale_win[:].bitcast(I32), 0)
+        nc.sync.dma_start(offsets[:], offs)
+        nc.sync.dma_start(w1_raw[:], w1.rearrange("(p t) r -> p (t r)", t=PACK))
+        scale_rows = tab_scales[0].rearrange("(q i) c -> i q c", i=4)
+        for i in range(4):
+            nc.scalar.dma_start(scale_win[i:P:32, :].bitcast(I32), scale_rows[i].bitcast(I32))
+        nc.sync.dma_start(word_win[:], tab_words[0].rearrange("p c t -> p (c t)").bitcast(I32))
+
+        def quantise(name, raw, cols, cast):
+            rounded = sb.tile([P, cols, PACK], BF16, name=name + "_bf", align_bytes=64)
+            codes = sb.tile([P, cols], U32, name=name + "_codes", align_bytes=64)
+            scales = sb.tile([P, cols], U8, name=name + "_scales", align_bytes=64)
+            cast(rounded[:], raw.rearrange("p (t c) -> p c t", t=PACK))
+            nc.vector.quantize_mx(out=codes[:].bitcast(FP8X4), scales=scales[:], in_=rounded[:].rearrange("p c t -> p (c t)"))
+            return codes, scales
+
+        w1_codes, w1_scales = quantise("w1", w1_raw[:], R, nc.vector.tensor_copy)
+
+        late = sb.tile([P, PACK * R + PACK * G + J + 16], F32, name="late", tag="stage")
+        wo_raw = late[:, 0 : PACK * R]
+        dy_raw = late[:, PACK * R : PACK * (R + G)]
+        base_sb = late[:, PACK * (R + G) : PACK * (R + G) + J]
+        share_sb = late[:, PACK * (R + G) + J : PACK * (R + G) + J + 1]
+        og_sb = late[:, PACK * (R + G) + J + 8 : PACK * (R + G) + J + 9]
+        nc.sync.dma_start(wo_raw, wo.rearrange("(p t) r -> p (t r)", t=PACK))
+        nc.sync.dma_start(dy_raw, dy.rearrange("(p t) g -> p (t g)", t=PACK))
+        nc.sync.dma_start(share_sb, share)
+        nc.sync.dma_start(og_sb, og)
+        nc.sync.dma_start(base_sb, base)
+
+        tab_sc = sb.tile([P, J], U8, name="tab_sc", align_bytes=64)
+        nc.vector.tensor_copy(tab_sc[:], scale_win[:].indirect(offsets[:]))
+
+        a_ps = []
+        for h in range(HALVES):
+            words = sb.tile([P, JH], U32, name="tab_w%d" % h, align_bytes=64)
+            nc.vector.tensor_copy(words[:], word_win[:].bitcast(U32).indirect(offsets[:, h * JH // 16 : (h + 1) * JH // 16]))
+            bank = psum.tile([P, JH], F32, name="a_ps%d" % h)
+            nc.tensor.matmul_mx(
+                out=bank[:],
+                lhsT=w1_codes[:].bitcast(FP8X4),
+                lhsT_scale=w1_scales[:],
+                rhs=words[:].bitcast(FP8X4),
+                rhs_scale=tab_sc[:, h * JH : (h + 1) * JH],
+                start=True,
+                stop=True,
+            )
+            a_ps.append(bank)
+
+        s1 = small("s1")
+        s2 = small("s2")
+        for h in range(HALVES):
+            cols = slice(h * GH, (h + 1) * GH)
+            sq = small("sq%d" % h, JH)
+            nc.scalar.activation(sq[:], a_ps[h][:], ACT.Square)
+            nc.vector.tensor_reduce(s1[:, cols], grouped(a_ps[h][:]), AX.X, add)
+            nc.vector.tensor_reduce(s2[:, cols], grouped(sq[:]), AX.X, add)
+
+        nq = small("nq")
+        nc.vector.scalar_tensor_tensor(nq[:], s1[:], -1.0 / POOL, s1[:], mult, mult)
+        var8 = small("var8")
+        nc.vector.tensor_tensor(var8[:], s2[:], nq[:], add)
+        y = small("y")
+        nc.scalar.activation(y[:], var8[:], ACT.Abs_reciprocal_sqrt, bias=EPS, scale=1.0 / POOL)
+
+        s8 = small("s8")
+        nc.vector.scalar_tensor_tensor(s8[:], var8[:], POOL * EPS, y[:], add, mult)
+        x8 = small("x8")
+        nc.vector.scalar_tensor_tensor(x8[:], s1[:], share_sb, s8[:], mult, add)
+        u = small("u")
+        nc.scalar.activation(u[:], x8[:], ACT.Tanh, scale=1.0 / POOL)
+
+        wo_codes, wo_scales = quantise("wo", wo_raw, R, nc.scalar.copy)
+        dy_codes, dy_scales = quantise("dy", dy_raw, G, nc.scalar.copy)
+        c_ps = psum.tile([P, G], F32, name="c_ps")
+        nc.tensor.matmul_mx(
+            out=c_ps[:],
+            lhsT=wo_codes[:].bitcast(FP8X4),
+            lhsT_scale=wo_scales[:],
+            rhs=dy_codes[:].bitcast(FP8X4),
+            rhs_scale=dy_scales[:],
+            start=True,
+            stop=True,
+        )
+        k1 = small("k1", 1)
+        nc.vector.tensor_scalar(k1[:], share_sb, share_sb, 1.0, mult, add)
+        cg = small("cg")
+        nc.vector.tensor_scalar(cg[:], c_ps[:], og_sb, 1.0 / 16, mult, mult)
+        cc = small("cc")
+        nc.vector.tensor_tensor(cc[:], c_ps[:], cg[:], mult)
+
+        y2 = small("y2")
+        nc.vector.tensor_tensor(y2[:], y[:], y[:], mult)
+        nmy = small("nmy")
+        nc.vector.scalar_tensor_tensor(nmy[:], s1[:], -1.0 / POOL, y[:], mult, mult)
+        hh = small("hh")
+        nc.vector.tensor_scalar(hh[:], y2[:], -EPS, k1[:], mult, add)
+        y4 = small("y4")
+        nc.vector.scalar_tensor_tensor(y4[:], y2[:], EPS / 2, y2[:], mult, mult)
+        ch = small("ch")
+        nc.vector.tensor_tensor(ch[:], cc[:], hh[:], mult)
+        fixed = sb.tile([P, 2, G], F32, name="fixed")
+        slope = sb.tile([P, 2, G], F32, name="slope")
+        nc.vector.tensor_tensor(fixed[:, 0, :], y4[:], cc[:], mult)
+        nc.vector.tensor_tensor(slope[:, 0, :], ch[:], y[:], mult)
+        nc.vector.scalar_tensor_tensor(slope[:, 1, :], nmy[:], share_sb, ch[:], add, mult)
+        nc.vector.scalar_tensor_tensor(fixed[:, 1, :], s1[:], -1.0 / POOL, fixed[:, 0, :], mult, mult)
+
+        u2 = small("u2")
+        nc.scalar.activation(u2[:], u[:], ACT.Square)
+        w2 = small("w2")
+        nc.scalar.activation(w2[:], u2[:], ACT.Square, bias=1.0, scale=-1.0)
+        us = sb.tile([P, 2, G], F32, name="us")
+        nc.vector.tensor_tensor(us[:], slope[:], u[:].unsqueeze(1).to_broadcast([P, 2, G]), mult)
+        inner = sb.tile([P, 2, G], F32, name="inner")
+        nc.vector.tensor_tensor(inner[:], fixed[:], us[:], sub)
+        coef = sb.tile([P, 2, G], F32, name="coef")
+        nc.vector.tensor_tensor(coef[:], inner[:], w2[:].unsqueeze(1).to_broadcast([P, 2, G]), mult)
+
+        for h in range(HALVES):
+            cols = slice(h * JH, (h + 1) * JH)
+            sc = small("scaled%d" % h, JH)
+            nc.vector.tensor_tensor(grouped(sc[:]), grouped(a_ps[h][:]), spread(coef[:, 0, :], h), mult)
+            sh = small("shifted%d" % h, JH)
+            nc.vector.tensor_tensor(grouped(sh[:]), grouped(base_sb[:, cols]), spread(coef[:, 1, :], h), add)
+            res = small("res%d" % h, JH)
+            nc.vector.tensor_tensor(res[:], sc[:], sh[:], add)
+            nc.sync.dma_start(out[:, cols], res[:])

@@ -23,6 +23,9 @@ EPS = 0.05
 HALVES = 2
 JH = J // HALVES
 GH = G // HALVES
+PIECES = 4
+JP = J // PIECES
+GP = G // PIECES
 
 
 def tile_attend_gpspreadpool_kernel(tc, tab_words, tab_scales, w1, share, wo, dy, og, base, offs, out):
@@ -36,8 +39,8 @@ def tile_attend_gpspreadpool_kernel(tc, tab_words, tab_scales, w1, share, wo, dy
         def small(name, cols=G):
             return sb.tile([P, cols], F32, name=name)
 
-        def spread(ap, h):
-            return ap[:, h * GH : (h + 1) * GH].unsqueeze(2).to_broadcast([P, GH, POOL])
+        def spread(ap):
+            return ap.unsqueeze(2).to_broadcast([P, ap.shape[1], POOL])
 
         def grouped(ap):
             return ap.rearrange("p (g i) -> p g i", i=POOL)
@@ -45,67 +48,73 @@ def tile_attend_gpspreadpool_kernel(tc, tab_words, tab_scales, w1, share, wo, dy
         offsets = sb.tile([P, J // 16], U16, name="offsets")
         scale_win = sb.tile([P, T], U8, name="scale_win")
         word_win = sb.tile([P, T], I32, name="word_win")
-        w1_raw = sb.tile([P, PACK * R], F32, name="w1_raw", tag="stage")
+        w1_raw = sb.tile([P, PACK, R], F32, name="w1_raw")
+        wo_raw = sb.tile([P, PACK, R], F32, name="wo_raw")
+        dy_raw = sb.tile([P, PACK, G], F32, name="dy_raw")
+        base_sb = sb.tile([P, J], F32, name="base_sb")
+        share_sb = small("share_sb", 1)
+        og_sb = small("og_sb", 1)
 
         nc.vector.memset(scale_win[:].bitcast(I32), 0)
+        warm_in = small("warm_in", 1)
+        warm_out = small("warm_out", 1)
+        nc.gpsimd.memset(warm_in[:], 1.0)
+        nc.scalar.activation(warm_out[:], warm_in[:], ACT.Abs_reciprocal_sqrt)
         nc.sync.dma_start(offsets[:], offs)
-        nc.sync.dma_start(w1_raw[:], w1.rearrange("(p t) r -> p (t r)", t=PACK))
+        nc.sync.dma_start(w1_raw[:], w1.rearrange("(p t) r -> p t r", t=PACK))
         scale_rows = tab_scales[0].rearrange("(q i) c -> i q c", i=4)
         for i in range(4):
-            nc.scalar.dma_start(scale_win[i:P:32, :].bitcast(I32), scale_rows[i].bitcast(I32))
+            nc.sync.dma_start(scale_win[i:P:32, :].bitcast(I32), scale_rows[i].bitcast(I32))
         nc.sync.dma_start(word_win[:], tab_words[0].rearrange("p c t -> p (c t)").bitcast(I32))
+        nc.sync.dma_start(dy_raw[:], dy.rearrange("(p t) g -> p t g", t=PACK))
+        nc.sync.dma_start(wo_raw[:], wo.rearrange("(p t) r -> p t r", t=PACK))
+        nc.sync.dma_start(share_sb[:], share)
+        nc.sync.dma_start(og_sb[:], og)
+        nc.sync.dma_start(base_sb[:], base)
 
-        def quantise(name, raw, cols, cast):
-            rounded = sb.tile([P, cols, PACK], BF16, name=name + "_bf", align_bytes=64)
-            codes = sb.tile([P, cols], U32, name=name + "_codes", align_bytes=64)
+        def quantise(name, raw, cols, cast, rounded_tag, codes_tag):
+            rounded = sb.tile([P, cols, PACK], BF16, name=name + "_bf", tag=rounded_tag, align_bytes=64)
+            codes = sb.tile([P, cols], U32, name=name + "_codes", tag=codes_tag, align_bytes=64)
             scales = sb.tile([P, cols], U8, name=name + "_scales", align_bytes=64)
-            cast(rounded[:], raw.rearrange("p (t c) -> p c t", t=PACK))
+            cast(
+                rounded[:].rearrange("p (c i) t -> p c t i", i=4),
+                raw[:].rearrange("p t (c i) -> p c t i", i=4),
+            )
             nc.vector.quantize_mx(out=codes[:].bitcast(FP8X4), scales=scales[:], in_=rounded[:].rearrange("p c t -> p (c t)"))
             return codes, scales
 
-        w1_codes, w1_scales = quantise("w1", w1_raw[:], R, nc.vector.tensor_copy)
-
-        late = sb.tile([P, PACK * R + PACK * G + J + 16], F32, name="late", tag="stage")
-        wo_raw = late[:, 0 : PACK * R]
-        dy_raw = late[:, PACK * R : PACK * (R + G)]
-        base_sb = late[:, PACK * (R + G) : PACK * (R + G) + J]
-        share_sb = late[:, PACK * (R + G) + J : PACK * (R + G) + J + 1]
-        og_sb = late[:, PACK * (R + G) + J + 8 : PACK * (R + G) + J + 9]
-        nc.sync.dma_start(wo_raw, wo.rearrange("(p t) r -> p (t r)", t=PACK))
-        nc.sync.dma_start(dy_raw, dy.rearrange("(p t) g -> p (t g)", t=PACK))
-        nc.sync.dma_start(share_sb, share)
-        nc.sync.dma_start(og_sb, og)
-        nc.sync.dma_start(base_sb, base)
+        w1_codes, w1_scales = quantise("w1", w1_raw, R, nc.vector.tensor_copy, "w1_bf", "w1_codes")
 
         tab_sc = sb.tile([P, J], U8, name="tab_sc", align_bytes=64)
         nc.vector.tensor_copy(tab_sc[:], scale_win[:].indirect(offsets[:]))
 
         a_ps = []
-        for h in range(HALVES):
-            words = sb.tile([P, JH], U32, name="tab_w%d" % h, align_bytes=64)
-            nc.vector.tensor_copy(words[:], word_win[:].bitcast(U32).indirect(offsets[:, h * JH // 16 : (h + 1) * JH // 16]))
-            bank = psum.tile([P, JH], F32, name="a_ps%d" % h)
+        for q in range(PIECES):
+            words = sb.tile([P, JP], U32, name="tab_w%d" % q, align_bytes=64)
+            nc.vector.tensor_copy(words[:], word_win[:].bitcast(U32).indirect(offsets[:, q * JP // 16 : (q + 1) * JP // 16]))
+            bank = psum.tile([P, JP], F32, name="a_ps%d" % q)
             nc.tensor.matmul_mx(
                 out=bank[:],
                 lhsT=w1_codes[:].bitcast(FP8X4),
                 lhsT_scale=w1_scales[:],
                 rhs=words[:].bitcast(FP8X4),
-                rhs_scale=tab_sc[:, h * JH : (h + 1) * JH],
+                rhs_scale=tab_sc[:, q * JP : (q + 1) * JP],
                 start=True,
                 stop=True,
             )
             a_ps.append(bank)
 
         s1 = small("s1")
-        s2 = small("s2")
+        s2 = sb.tile([P, G], F32, name="s2", tag="s2_dy", align_bytes=64)
+        sq = small("sq", J)
+        for q in range(PIECES):
+            nc.scalar.activation(sq[:, q * JP : (q + 1) * JP], a_ps[q][:], ACT.Square)
         for h in range(HALVES):
-            cols = slice(h * GH, (h + 1) * GH)
-            sq = small("sq%d" % h, JH)
-            nc.scalar.activation(sq[:], a_ps[h][:], ACT.Square)
-            nc.vector.tensor_reduce(s1[:, cols], grouped(a_ps[h][:]), AX.X, add)
-            nc.vector.tensor_reduce(s2[:, cols], grouped(sq[:]), AX.X, add)
+            for q in range(h * PIECES // HALVES, (h + 1) * PIECES // HALVES):
+                nc.vector.tensor_reduce(s1[:, q * GP : (q + 1) * GP], grouped(a_ps[q][:]), AX.X, add)
+            nc.vector.tensor_reduce(s2[:, h * GH : (h + 1) * GH], grouped(sq[:, h * JH : (h + 1) * JH]), AX.X, add)
 
-        nq = small("nq")
+        nq = sb.tile([P, G], F32, name="nq", tag="nq_wo", align_bytes=64)
         nc.vector.scalar_tensor_tensor(nq[:], s1[:], -1.0 / POOL, s1[:], mult, mult)
         var8 = small("var8")
         nc.vector.tensor_tensor(var8[:], s2[:], nq[:], add)
@@ -115,12 +124,12 @@ def tile_attend_gpspreadpool_kernel(tc, tab_words, tab_scales, w1, share, wo, dy
         s8 = small("s8")
         nc.vector.scalar_tensor_tensor(s8[:], var8[:], POOL * EPS, y[:], add, mult)
         x8 = small("x8")
-        nc.vector.scalar_tensor_tensor(x8[:], s1[:], share_sb, s8[:], mult, add)
+        nc.vector.scalar_tensor_tensor(x8[:], s1[:], share_sb[:], s8[:], mult, add)
         u = small("u")
         nc.scalar.activation(u[:], x8[:], ACT.Tanh, scale=1.0 / POOL)
 
-        wo_codes, wo_scales = quantise("wo", wo_raw, R, nc.scalar.copy)
-        dy_codes, dy_scales = quantise("dy", dy_raw, G, nc.scalar.copy)
+        wo_codes, wo_scales = quantise("wo", wo_raw, R, nc.scalar.copy, "w1_codes", "nq_wo")
+        dy_codes, dy_scales = quantise("dy", dy_raw, G, nc.scalar.copy, "dy_bf", "s2_dy")
         c_ps = psum.tile([P, G], F32, name="c_ps")
         nc.tensor.matmul_mx(
             out=c_ps[:],
@@ -132,9 +141,9 @@ def tile_attend_gpspreadpool_kernel(tc, tab_words, tab_scales, w1, share, wo, dy
             stop=True,
         )
         k1 = small("k1", 1)
-        nc.vector.tensor_scalar(k1[:], share_sb, share_sb, 1.0, mult, add)
+        nc.gpsimd.tensor_scalar(k1[:], share_sb[:], share_sb[:], 1.0, mult, add)
         cg = small("cg")
-        nc.vector.tensor_scalar(cg[:], c_ps[:], og_sb, 1.0 / 16, mult, mult)
+        nc.vector.tensor_scalar(cg[:], c_ps[:], og_sb[:], 1.0 / 16, mult, mult)
         cc = small("cc")
         nc.vector.tensor_tensor(cc[:], c_ps[:], cg[:], mult)
 
@@ -144,34 +153,48 @@ def tile_attend_gpspreadpool_kernel(tc, tab_words, tab_scales, w1, share, wo, dy
         nc.vector.scalar_tensor_tensor(nmy[:], s1[:], -1.0 / POOL, y[:], mult, mult)
         hh = small("hh")
         nc.vector.tensor_scalar(hh[:], y2[:], -EPS, k1[:], mult, add)
-        y4 = small("y4")
-        nc.vector.scalar_tensor_tensor(y4[:], y2[:], EPS / 2, y2[:], mult, mult)
-        ch = small("ch")
-        nc.vector.tensor_tensor(ch[:], cc[:], hh[:], mult)
-        fixed = sb.tile([P, 2, G], F32, name="fixed")
-        slope = sb.tile([P, 2, G], F32, name="slope")
-        nc.vector.tensor_tensor(fixed[:, 0, :], y4[:], cc[:], mult)
-        nc.vector.tensor_tensor(slope[:, 0, :], ch[:], y[:], mult)
-        nc.vector.scalar_tensor_tensor(slope[:, 1, :], nmy[:], share_sb, ch[:], add, mult)
-        nc.vector.scalar_tensor_tensor(fixed[:, 1, :], s1[:], -1.0 / POOL, fixed[:, 0, :], mult, mult)
+        raw_terms = sb.tile([P, 4, G], F32, name="raw_terms")
+        nc.vector.scalar_tensor_tensor(raw_terms[:, 0, :], y2[:], EPS / 2, y2[:], mult, mult)
+        nc.vector.tensor_tensor(raw_terms[:, 2, :], hh[:], y[:], mult)
+        nc.vector.scalar_tensor_tensor(raw_terms[:, 3, :], nmy[:], share_sb[:], hh[:], add, mult)
+        nc.vector.scalar_tensor_tensor(raw_terms[:, 1, :], s1[:], -1.0 / POOL, raw_terms[:, 0, :], mult, mult)
+        terms = sb.tile([P, 4, G], F32, name="terms")
+        for j in (2, 0):
+            nc.vector.tensor_tensor(terms[:, j : j + 2, :], raw_terms[:, j : j + 2, :], cc[:].unsqueeze(1).to_broadcast([P, 2, G]), mult)
 
         u2 = small("u2")
         nc.scalar.activation(u2[:], u[:], ACT.Square)
         w2 = small("w2")
         nc.scalar.activation(w2[:], u2[:], ACT.Square, bias=1.0, scale=-1.0)
         us = sb.tile([P, 2, G], F32, name="us")
-        nc.vector.tensor_tensor(us[:], slope[:], u[:].unsqueeze(1).to_broadcast([P, 2, G]), mult)
         inner = sb.tile([P, 2, G], F32, name="inner")
-        nc.vector.tensor_tensor(inner[:], fixed[:], us[:], sub)
         coef = sb.tile([P, 2, G], F32, name="coef")
-        nc.vector.tensor_tensor(coef[:], inner[:], w2[:].unsqueeze(1).to_broadcast([P, 2, G]), mult)
+        for j in (1, 0):
+            nc.vector.tensor_tensor(us[:, j, :], terms[:, 2 + j, :], u[:], mult)
+        for j in (1, 0):
+            nc.vector.tensor_tensor(inner[:, j, :], terms[:, j, :], us[:, j, :], sub)
+        for j in (1, 0):
+            nc.vector.tensor_tensor(coef[:, j, :], inner[:, j, :], w2[:], mult)
 
+        last = PIECES - 1
+        JV = last * JP
+        scaled = small("scaled", J)
+        for g in range(GP):
+            gg = last * GP + g
+            nc.scalar.activation(
+                scaled[:, gg * POOL : (gg + 1) * POOL],
+                a_ps[last][:, g * POOL : (g + 1) * POOL],
+                ACT.Identity,
+                bias=coef[:, 1, gg : gg + 1],
+                scale=coef[:, 0, gg : gg + 1],
+            )
+        res = small("res", J)
+        nc.vector.tensor_tensor(grouped(base_sb[:, 0:JV]), grouped(base_sb[:, 0:JV]), spread(coef[:, 1, 0 : last * GP]), add)
+        for q in range(last):
+            nc.vector.tensor_tensor(
+                grouped(scaled[:, q * JP : (q + 1) * JP]), grouped(a_ps[q][:]), spread(coef[:, 0, q * GP : (q + 1) * GP]), mult
+            )
         for h in range(HALVES):
             cols = slice(h * JH, (h + 1) * JH)
-            sc = small("scaled%d" % h, JH)
-            nc.vector.tensor_tensor(grouped(sc[:]), grouped(a_ps[h][:]), spread(coef[:, 0, :], h), mult)
-            sh = small("shifted%d" % h, JH)
-            nc.vector.tensor_tensor(grouped(sh[:]), grouped(base_sb[:, cols]), spread(coef[:, 1, :], h), add)
-            res = small("res%d" % h, JH)
-            nc.vector.tensor_tensor(res[:], sc[:], sh[:], add)
-            nc.sync.dma_start(out[:, cols], res[:])
+            nc.vector.tensor_tensor(res[:, cols], scaled[:, cols], base_sb[:, cols], add)
+            nc.sync.dma_start(out[:, cols], res[:, cols])

@@ -47,7 +47,7 @@ def tile_attend_gpspreadpool_kernel(tc, tab_words, tab_scales, w1, share, wo, dy
 
         offsets = sb.tile([P, J // 16], U16, name="offsets")
         scale_win = sb.tile([P, T], U8, name="scale_win")
-        word_win = sb.tile([P, T], I32, name="word_win")
+        word_win = sb.tile([P, T], I32, name="word_win", align_bytes=64)
         w1_raw = sb.tile([P, PACK, R], F32, name="w1_raw")
         wo_raw = sb.tile([P, PACK, R], F32, name="wo_raw")
         dy_raw = sb.tile([P, PACK, G], F32, name="dy_raw")
@@ -60,14 +60,14 @@ def tile_attend_gpspreadpool_kernel(tc, tab_words, tab_scales, w1, share, wo, dy
         warm_out = small("warm_out", 1)
         nc.gpsimd.memset(warm_in[:], 1.0)
         nc.scalar.activation(warm_out[:], warm_in[:], ACT.Abs_reciprocal_sqrt)
-        nc.sync.dma_start(offsets[:], offs)
         nc.sync.dma_start(w1_raw[:], w1.rearrange("(p t) r -> p t r", t=PACK))
+        nc.sync.dma_start(offsets[:], offs)
         scale_rows = tab_scales[0].rearrange("(q i) c -> i q c", i=4)
         for i in range(4):
             nc.sync.dma_start(scale_win[i:P:32, :].bitcast(I32), scale_rows[i].bitcast(I32))
         nc.sync.dma_start(word_win[:], tab_words[0].rearrange("p c t -> p (c t)").bitcast(I32))
-        nc.sync.dma_start(dy_raw[:], dy.rearrange("(p t) g -> p t g", t=PACK))
         nc.sync.dma_start(wo_raw[:], wo.rearrange("(p t) r -> p t r", t=PACK))
+        nc.sync.dma_start(dy_raw[:], dy.rearrange("(p t) g -> p t g", t=PACK))
         nc.sync.dma_start(share_sb[:], share)
         nc.sync.dma_start(og_sb[:], og)
         nc.sync.dma_start(base_sb[:], base)
@@ -114,8 +114,10 @@ def tile_attend_gpspreadpool_kernel(tc, tab_words, tab_scales, w1, share, wo, dy
                 nc.vector.tensor_reduce(s1[:, q * GP : (q + 1) * GP], grouped(a_ps[q][:]), AX.X, add)
             nc.vector.tensor_reduce(s2[:, h * GH : (h + 1) * GH], grouped(sq[:, h * JH : (h + 1) * JH]), AX.X, add)
 
-        nq = sb.tile([P, G], F32, name="nq", tag="nq_wo", align_bytes=64)
+        nq = small("nq")
         nc.vector.scalar_tensor_tensor(nq[:], s1[:], -1.0 / POOL, s1[:], mult, mult)
+        a_last = small("a_last", JP)
+        nc.scalar.copy(a_last[:], a_ps[PIECES - 1][:])
         var8 = small("var8")
         nc.vector.tensor_tensor(var8[:], s2[:], nq[:], add)
         y = small("y")
@@ -128,8 +130,8 @@ def tile_attend_gpspreadpool_kernel(tc, tab_words, tab_scales, w1, share, wo, dy
         u = small("u")
         nc.scalar.activation(u[:], x8[:], ACT.Tanh, scale=1.0 / POOL)
 
-        wo_codes, wo_scales = quantise("wo", wo_raw, R, nc.scalar.copy, "w1_codes", "nq_wo")
-        dy_codes, dy_scales = quantise("dy", dy_raw, G, nc.scalar.copy, "dy_bf", "s2_dy")
+        wo_codes, wo_scales = quantise("wo", wo_raw, R, nc.vector.tensor_copy, "word_win", "wo_codes")
+        dy_codes, dy_scales = quantise("dy", dy_raw, G, nc.scalar.copy, "w1_codes", "s2_dy")
         c_ps = psum.tile([P, G], F32, name="c_ps")
         nc.tensor.matmul_mx(
             out=c_ps[:],
@@ -141,7 +143,7 @@ def tile_attend_gpspreadpool_kernel(tc, tab_words, tab_scales, w1, share, wo, dy
             stop=True,
         )
         k1 = small("k1", 1)
-        nc.gpsimd.tensor_scalar(k1[:], share_sb[:], share_sb[:], 1.0, mult, add)
+        nc.vector.tensor_scalar(k1[:], share_sb[:], share_sb[:], 1.0, mult, add)
         cg = small("cg")
         nc.vector.tensor_scalar(cg[:], c_ps[:], og_sb[:], 1.0 / 16, mult, mult)
         cc = small("cc")
@@ -183,7 +185,7 @@ def tile_attend_gpspreadpool_kernel(tc, tab_words, tab_scales, w1, share, wo, dy
             gg = last * GP + g
             nc.scalar.activation(
                 scaled[:, gg * POOL : (gg + 1) * POOL],
-                a_ps[last][:, g * POOL : (g + 1) * POOL],
+                a_last[:, g * POOL : (g + 1) * POOL],
                 ACT.Identity,
                 bias=coef[:, 1, gg : gg + 1],
                 scale=coef[:, 0, gg : gg + 1],
@@ -194,7 +196,6 @@ def tile_attend_gpspreadpool_kernel(tc, tab_words, tab_scales, w1, share, wo, dy
             nc.vector.tensor_tensor(
                 grouped(scaled[:, q * JP : (q + 1) * JP]), grouped(a_ps[q][:]), spread(coef[:, 0, q * GP : (q + 1) * GP]), mult
             )
-        for h in range(HALVES):
-            cols = slice(h * JH, (h + 1) * JH)
+        for cols in (slice(0, JH), slice(JH, JV), slice(JV, J)):
             nc.vector.tensor_tensor(res[:, cols], scaled[:, cols], base_sb[:, cols], add)
             nc.sync.dma_start(out[:, cols], res[:, cols])

@@ -18,14 +18,20 @@ AX = mybir.AxisListType
 
 P = 128
 PACK = 4
+QUADRANT = 32
+SCALE_ROWS = 4
+LIST_ROWS = 16
+RUN = 4
 POOL = J // G
 EPS = 0.05
-HALVES = 2
-JH = J // HALVES
-GH = G // HALVES
+GAIN, OFFSET = 0, 1
+
 PIECES = 4
-JP = J // PIECES
-GP = G // PIECES
+JP, GP = J // PIECES, G // PIECES
+LAST = PIECES - 1
+HALVES = 2
+JH, GH = J // HALVES, G // HALVES
+JV = LAST * JP
 
 
 def tile_attend_gpspreadpool_kernel(tc, tab_words, tab_scales, w1, share, wo, dy, og, base, offs, out):
@@ -36,35 +42,35 @@ def tile_attend_gpspreadpool_kernel(tc, tab_words, tab_scales, w1, share, wo, dy
         sb = ctx.enter_context(tc.tile_pool(name="sb", bufs=1))
         psum = ctx.enter_context(tc.psum_pool(name="psum", bufs=1))
 
-        def small(name, cols=G):
+        def floats(name, cols=G):
             return sb.tile([P, cols], F32, name=name)
 
-        def spread(ap):
-            return ap.unsqueeze(2).to_broadcast([P, ap.shape[1], POOL])
+        def spread(per_group):
+            return per_group.unsqueeze(2).to_broadcast([P, per_group.shape[1], POOL])
 
-        def grouped(ap):
-            return ap.rearrange("p (g i) -> p g i", i=POOL)
+        def grouped(per_slot):
+            return per_slot.rearrange("p (g i) -> p g i", i=POOL)
 
-        offsets = sb.tile([P, J // 16], U16, name="offsets")
+        offsets = sb.tile([P, J // LIST_ROWS], U16, name="offsets")
         scale_win = sb.tile([P, T], U8, name="scale_win")
         word_win = sb.tile([P, T], I32, name="word_win", align_bytes=64)
         w1_raw = sb.tile([P, PACK, R], F32, name="w1_raw")
         wo_raw = sb.tile([P, PACK, R], F32, name="wo_raw")
         dy_raw = sb.tile([P, PACK, G], F32, name="dy_raw")
         base_sb = sb.tile([P, J], F32, name="base_sb")
-        share_sb = small("share_sb", 1)
-        og_sb = small("og_sb", 1)
+        share_sb = floats("share_sb", 1)
+        og_sb = floats("og_sb", 1)
 
         nc.vector.memset(scale_win[:].bitcast(I32), 0)
-        warm_in = small("warm_in", 1)
-        warm_out = small("warm_out", 1)
+        warm_in = floats("warm_in", 1)
+        warm_out = floats("warm_out", 1)
         nc.gpsimd.memset(warm_in[:], 1.0)
         nc.scalar.activation(warm_out[:], warm_in[:], ACT.Abs_reciprocal_sqrt)
         nc.sync.dma_start(w1_raw[:], w1.rearrange("(p t) r -> p t r", t=PACK))
         nc.sync.dma_start(offsets[:], offs)
-        scale_rows = tab_scales[0].rearrange("(q i) c -> i q c", i=4)
-        for i in range(4):
-            nc.sync.dma_start(scale_win[i:P:32, :].bitcast(I32), scale_rows[i].bitcast(I32))
+        scale_rows = tab_scales[0].rearrange("(q i) c -> i q c", i=SCALE_ROWS)
+        for i in range(SCALE_ROWS):
+            nc.sync.dma_start(scale_win[i:P:QUADRANT, :].bitcast(I32), scale_rows[i].bitcast(I32))
         nc.sync.dma_start(word_win[:], tab_words[0].rearrange("p c t -> p (c t)").bitcast(I32))
         nc.sync.dma_start(wo_raw[:], wo.rearrange("(p t) r -> p t r", t=PACK))
         nc.sync.dma_start(dy_raw[:], dy.rearrange("(p t) g -> p t g", t=PACK))
@@ -77,8 +83,8 @@ def tile_attend_gpspreadpool_kernel(tc, tab_words, tab_scales, w1, share, wo, dy
             codes = sb.tile([P, cols], U32, name=name + "_codes", tag=codes_tag, align_bytes=64)
             scales = sb.tile([P, cols], U8, name=name + "_scales", align_bytes=64)
             cast(
-                rounded[:].rearrange("p (c i) t -> p c t i", i=4),
-                raw[:].rearrange("p t (c i) -> p c t i", i=4),
+                rounded[:].rearrange("p (c i) t -> p c t i", i=RUN),
+                raw[:].rearrange("p t (c i) -> p c t i", i=RUN),
             )
             nc.vector.quantize_mx(out=codes[:].bitcast(FP8X4), scales=scales[:], in_=rounded[:].rearrange("p c t -> p (c t)"))
             return codes, scales
@@ -88,50 +94,56 @@ def tile_attend_gpspreadpool_kernel(tc, tab_words, tab_scales, w1, share, wo, dy
         tab_sc = sb.tile([P, J], U8, name="tab_sc", align_bytes=64)
         nc.vector.tensor_copy(tab_sc[:], scale_win[:].indirect(offsets[:]))
 
-        a_ps = []
+        a_ps, a_scalar = [], []
         for q in range(PIECES):
             words = sb.tile([P, JP], U32, name="tab_w%d" % q, align_bytes=64)
-            nc.vector.tensor_copy(words[:], word_win[:].bitcast(U32).indirect(offsets[:, q * JP // 16 : (q + 1) * JP // 16]))
-            bank = psum.tile([P, JP], F32, name="a_ps%d" % q)
-            nc.tensor.matmul_mx(
-                out=bank[:],
-                lhsT=w1_codes[:].bitcast(FP8X4),
-                lhsT_scale=w1_scales[:],
-                rhs=words[:].bitcast(FP8X4),
-                rhs_scale=tab_sc[:, q * JP : (q + 1) * JP],
-                start=True,
-                stop=True,
-            )
+            entries = offsets[:, q * JP // LIST_ROWS : (q + 1) * JP // LIST_ROWS]
+            nc.vector.tensor_copy(words[:], word_win[:].bitcast(U32).indirect(entries))
+            for copy in range(2 if q == LAST else 1):
+                bank = psum.tile([P, JP], F32, name="a_ps%d_%d" % (q, copy))
+                nc.tensor.matmul_mx(
+                    out=bank[:],
+                    lhsT=w1_codes[:].bitcast(FP8X4),
+                    lhsT_scale=w1_scales[:],
+                    rhs=words[:].bitcast(FP8X4),
+                    rhs_scale=tab_sc[:, q * JP : (q + 1) * JP],
+                    start=True,
+                    stop=True,
+                )
+                if copy == 0:
+                    a_scalar.append(bank)
             a_ps.append(bank)
 
-        s1 = small("s1")
-        s2 = sb.tile([P, G], F32, name="s2", tag="s2_dy", align_bytes=64)
-        sq = small("sq", J)
+        s1 = floats("s1")
+        s2 = floats("s2")
+        sq = [sb.tile([P, JH], F32, name="sq%d" % h, align_bytes=64) for h in range(HALVES)]
+        per_half = PIECES // HALVES
         for q in range(PIECES):
-            nc.scalar.activation(sq[:, q * JP : (q + 1) * JP], a_ps[q][:], ACT.Square)
+            place = q % per_half
+            nc.scalar.activation(sq[q // per_half][:, place * JP : (place + 1) * JP], a_scalar[q][:], ACT.Square)
         for h in range(HALVES):
-            for q in range(h * PIECES // HALVES, (h + 1) * PIECES // HALVES):
+            for q in range(h * per_half, (h + 1) * per_half):
                 nc.vector.tensor_reduce(s1[:, q * GP : (q + 1) * GP], grouped(a_ps[q][:]), AX.X, add)
-            nc.vector.tensor_reduce(s2[:, h * GH : (h + 1) * GH], grouped(sq[:, h * JH : (h + 1) * JH]), AX.X, add)
+            nc.vector.tensor_reduce(s2[:, h * GH : (h + 1) * GH], grouped(sq[h][:]), AX.X, add)
 
-        nq = small("nq")
+        nq = floats("nq")
         nc.vector.scalar_tensor_tensor(nq[:], s1[:], -1.0 / POOL, s1[:], mult, mult)
-        a_last = small("a_last", JP)
-        nc.scalar.copy(a_last[:], a_ps[PIECES - 1][:])
-        var8 = small("var8")
+        a_last = floats("a_last", JP)
+        nc.scalar.copy(a_last[:], a_scalar[LAST][:])
+        var8 = floats("var8")
         nc.vector.tensor_tensor(var8[:], s2[:], nq[:], add)
-        y = small("y")
+        y = floats("y")
         nc.scalar.activation(y[:], var8[:], ACT.Abs_reciprocal_sqrt, bias=EPS, scale=1.0 / POOL)
 
-        s8 = small("s8")
+        s8 = floats("s8")
         nc.vector.scalar_tensor_tensor(s8[:], var8[:], POOL * EPS, y[:], add, mult)
-        x8 = small("x8")
+        x8 = floats("x8")
         nc.vector.scalar_tensor_tensor(x8[:], s1[:], share_sb[:], s8[:], mult, add)
-        u = small("u")
+        u = floats("u")
         nc.scalar.activation(u[:], x8[:], ACT.Tanh, scale=1.0 / POOL)
 
         wo_codes, wo_scales = quantise("wo", wo_raw, R, nc.vector.tensor_copy, "word_win", "wo_codes")
-        dy_codes, dy_scales = quantise("dy", dy_raw, G, nc.scalar.copy, "w1_codes", "s2_dy")
+        dy_codes, dy_scales = quantise("dy", dy_raw, G, nc.scalar.copy, "w1_codes", "sq1")
         c_ps = psum.tile([P, G], F32, name="c_ps")
         nc.tensor.matmul_mx(
             out=c_ps[:],
@@ -142,59 +154,58 @@ def tile_attend_gpspreadpool_kernel(tc, tab_words, tab_scales, w1, share, wo, dy
             start=True,
             stop=True,
         )
-        k1 = small("k1", 1)
-        nc.vector.tensor_scalar(k1[:], share_sb[:], share_sb[:], 1.0, mult, add)
-        cg = small("cg")
-        nc.vector.tensor_scalar(cg[:], c_ps[:], og_sb[:], 1.0 / 16, mult, mult)
-        cc = small("cc")
+        h_top = floats("h_top", 1)
+        nc.vector.tensor_scalar(h_top[:], share_sb[:], share_sb[:], 1.0, mult, add)
+        cg = floats("cg")
+        nc.vector.tensor_scalar(cg[:], c_ps[:], og_sb[:], 1.0 / (2 * POOL), mult, mult)
+        cc = floats("cc")
         nc.vector.tensor_tensor(cc[:], c_ps[:], cg[:], mult)
 
-        y2 = small("y2")
+        y2 = floats("y2")
         nc.vector.tensor_tensor(y2[:], y[:], y[:], mult)
-        nmy = small("nmy")
+        nmy = floats("nmy")
         nc.vector.scalar_tensor_tensor(nmy[:], s1[:], -1.0 / POOL, y[:], mult, mult)
-        hh = small("hh")
-        nc.vector.tensor_scalar(hh[:], y2[:], -EPS, k1[:], mult, add)
+        hh = floats("hh")
+        nc.vector.tensor_scalar(hh[:], y2[:], -EPS, h_top[:], mult, add)
+        fixed, slope = 0, 2
         raw_terms = sb.tile([P, 4, G], F32, name="raw_terms")
-        nc.vector.scalar_tensor_tensor(raw_terms[:, 0, :], y2[:], EPS / 2, y2[:], mult, mult)
-        nc.vector.tensor_tensor(raw_terms[:, 2, :], hh[:], y[:], mult)
-        nc.vector.scalar_tensor_tensor(raw_terms[:, 3, :], nmy[:], share_sb[:], hh[:], add, mult)
-        nc.vector.scalar_tensor_tensor(raw_terms[:, 1, :], s1[:], -1.0 / POOL, raw_terms[:, 0, :], mult, mult)
+        nc.vector.scalar_tensor_tensor(raw_terms[:, fixed + GAIN, :], y2[:], EPS / 2, y2[:], mult, mult)
+        nc.vector.tensor_tensor(raw_terms[:, slope + GAIN, :], hh[:], y[:], mult)
+        nc.vector.scalar_tensor_tensor(raw_terms[:, slope + OFFSET, :], nmy[:], share_sb[:], hh[:], add, mult)
+        nc.vector.scalar_tensor_tensor(raw_terms[:, fixed + OFFSET, :], s1[:], -1.0 / POOL, raw_terms[:, fixed + GAIN, :], mult, mult)
         terms = sb.tile([P, 4, G], F32, name="terms")
-        for j in (2, 0):
+        for j in (slope, fixed):
             nc.vector.tensor_tensor(terms[:, j : j + 2, :], raw_terms[:, j : j + 2, :], cc[:].unsqueeze(1).to_broadcast([P, 2, G]), mult)
 
-        u2 = small("u2")
+        u2 = floats("u2")
         nc.scalar.activation(u2[:], u[:], ACT.Square)
-        w2 = small("w2")
+        w2 = floats("w2")
         nc.scalar.activation(w2[:], u2[:], ACT.Square, bias=1.0, scale=-1.0)
         us = sb.tile([P, 2, G], F32, name="us")
         inner = sb.tile([P, 2, G], F32, name="inner")
         coef = sb.tile([P, 2, G], F32, name="coef")
-        for j in (1, 0):
-            nc.vector.tensor_tensor(us[:, j, :], terms[:, 2 + j, :], u[:], mult)
-        for j in (1, 0):
-            nc.vector.tensor_tensor(inner[:, j, :], terms[:, j, :], us[:, j, :], sub)
-        for j in (1, 0):
+        for j in (OFFSET, GAIN):
+            nc.vector.tensor_tensor(us[:, j, :], terms[:, slope + j, :], u[:], mult)
+        for j in (OFFSET, GAIN):
+            nc.vector.tensor_tensor(inner[:, j, :], terms[:, fixed + j, :], us[:, j, :], sub)
+        for j in (OFFSET, GAIN):
             nc.vector.tensor_tensor(coef[:, j, :], inner[:, j, :], w2[:], mult)
 
-        last = PIECES - 1
-        JV = last * JP
-        scaled = small("scaled", J)
+        scaled = floats("scaled", J)
         for g in range(GP):
-            gg = last * GP + g
+            group = LAST * GP + g
             nc.scalar.activation(
-                scaled[:, gg * POOL : (gg + 1) * POOL],
+                scaled[:, group * POOL : (group + 1) * POOL],
                 a_last[:, g * POOL : (g + 1) * POOL],
                 ACT.Identity,
-                bias=coef[:, 1, gg : gg + 1],
-                scale=coef[:, 0, gg : gg + 1],
+                bias=coef[:, OFFSET, group : group + 1],
+                scale=coef[:, GAIN, group : group + 1],
             )
-        res = small("res", J)
-        nc.vector.tensor_tensor(grouped(base_sb[:, 0:JV]), grouped(base_sb[:, 0:JV]), spread(coef[:, 1, 0 : last * GP]), add)
-        for q in range(last):
+        res = floats("res", J)
+        nc.vector.tensor_tensor(grouped(base_sb[:, 0:JV]), grouped(base_sb[:, 0:JV]), spread(coef[:, OFFSET, 0 : LAST * GP]), add)
+        for q in range(LAST):
             nc.vector.tensor_tensor(
-                grouped(scaled[:, q * JP : (q + 1) * JP]), grouped(a_ps[q][:]), spread(coef[:, 0, q * GP : (q + 1) * GP]), mult
+                grouped(scaled[:, q * JP : (q + 1) * JP]), grouped(a_ps[q][:]), spread(coef[:, GAIN, q * GP : (q + 1) * GP]), mult
             )
         for cols in (slice(0, JH), slice(JH, JV), slice(JV, J)):
             nc.vector.tensor_tensor(res[:, cols], scaled[:, cols], base_sb[:, cols], add)

from contextlib import ExitStack

import concourse.mybir as mybir

K, R, F, T, J, G = 512, 128, 512, 2048, 512, 64
FLOPS = 2 * K * R * J + 2 * F * R * G

F32 = mybir.dt.float32
BF16 = mybir.dt.bfloat16
I32 = mybir.dt.int32
U32 = mybir.dt.uint32
U16 = mybir.dt.uint16
U8 = mybir.dt.uint8
FP8X4 = mybir.dt.float8_e4m3fn_x4
ALU = mybir.AluOpType
ACT = mybir.ActivationFunctionType
AX = mybir.AxisListType

P = 128
PACK = 4
QUADRANT = 32
SCALE_ROWS = 4
LIST_ROWS = 16
RUN = 4
POOL = J // G
EPS = 0.05
GAIN, OFFSET = 0, 1

PIECES = 4
JP, GP = J // PIECES, G // PIECES
LAST = PIECES - 1
HALVES = 2
JH, GH = J // HALVES, G // HALVES
JV = LAST * JP


def tile_attend_gpspreadpool_kernel(tc, tab_words, tab_scales, w1, share, wo, dy, og, base, offs, out):
    nc = tc.nc
    mult, add, sub = ALU.mult, ALU.add, ALU.subtract

    with ExitStack() as ctx:
        sb = ctx.enter_context(tc.tile_pool(name="sb", bufs=1))
        psum = ctx.enter_context(tc.psum_pool(name="psum", bufs=1))

        def floats(name, cols=G):
            return sb.tile([P, cols], F32, name=name)

        def spread(per_group):
            return per_group.unsqueeze(2).to_broadcast([P, per_group.shape[1], POOL])

        def grouped(per_slot):
            return per_slot.rearrange("p (g i) -> p g i", i=POOL)

        offsets = sb.tile([P, J // LIST_ROWS], U16, name="offsets")
        scale_win = sb.tile([P, T], U8, name="scale_win")
        word_win = sb.tile([P, T], I32, name="word_win", align_bytes=64)
        w1_raw = sb.tile([P, PACK, R], F32, name="w1_raw")
        wo_raw = sb.tile([P, PACK, R], F32, name="wo_raw")
        dy_raw = sb.tile([P, PACK, G], F32, name="dy_raw")
        base_sb = sb.tile([P, J], F32, name="base_sb")
        share_sb = floats("share_sb", 1)
        og_sb = floats("og_sb", 1)

        nc.vector.memset(scale_win[:].bitcast(I32), 0)
        warm_in = floats("warm_in", 1)
        warm_out = floats("warm_out", 1)
        nc.gpsimd.memset(warm_in[:], 1.0)
        nc.scalar.activation(warm_out[:], warm_in[:], ACT.Abs_reciprocal_sqrt)
        nc.sync.dma_start(w1_raw[:], w1.rearrange("(p t) r -> p t r", t=PACK))
        nc.sync.dma_start(offsets[:], offs)
        scale_rows = tab_scales[0].rearrange("(q i) c -> i q c", i=SCALE_ROWS)
        for i in range(SCALE_ROWS):
            nc.sync.dma_start(scale_win[i:P:QUADRANT, :].bitcast(I32), scale_rows[i].bitcast(I32))
        nc.sync.dma_start(word_win[:], tab_words[0].rearrange("p c t -> p (c t)").bitcast(I32))
        nc.sync.dma_start(wo_raw[:], wo.rearrange("(p t) r -> p t r", t=PACK))
        nc.sync.dma_start(dy_raw[:], dy.rearrange("(p t) g -> p t g", t=PACK))
        nc.sync.dma_start(share_sb[:], share)
        nc.sync.dma_start(og_sb[:], og)
        nc.sync.dma_start(base_sb[:], base)

        def quantise(name, raw, cols, cast, rounded_tag, codes_tag):
            rounded = sb.tile([P, cols, PACK], BF16, name=name + "_bf", tag=rounded_tag, align_bytes=64)
            codes = sb.tile([P, cols], U32, name=name + "_codes", tag=codes_tag, align_bytes=64)
            scales = sb.tile([P, cols], U8, name=name + "_scales", align_bytes=64)
            cast(
                rounded[:].rearrange("p (c i) t -> p c t i", i=RUN),
                raw[:].rearrange("p t (c i) -> p c t i", i=RUN),
            )
            nc.vector.quantize_mx(out=codes[:].bitcast(FP8X4), scales=scales[:], in_=rounded[:].rearrange("p c t -> p (c t)"))
            return codes, scales

        w1_codes, w1_scales = quantise("w1", w1_raw, R, nc.vector.tensor_copy, "w1_bf", "w1_codes")

        tab_sc = sb.tile([P, J], U8, name="tab_sc", align_bytes=64)
        nc.vector.tensor_copy(tab_sc[:], scale_win[:].indirect(offsets[:]))

        a_ps, a_scalar = [], []
        for q in range(PIECES):
            words = sb.tile([P, JP], U32, name="tab_w%d" % q, align_bytes=64)
            entries = offsets[:, q * JP // LIST_ROWS : (q + 1) * JP // LIST_ROWS]
            nc.vector.tensor_copy(words[:], word_win[:].bitcast(U32).indirect(entries))
            for copy in range(2 if q == LAST else 1):
                bank = psum.tile([P, JP], F32, name="a_ps%d_%d" % (q, copy))
                nc.tensor.matmul_mx(
                    out=bank[:],
                    lhsT=w1_codes[:].bitcast(FP8X4),
                    lhsT_scale=w1_scales[:],
                    rhs=words[:].bitcast(FP8X4),
                    rhs_scale=tab_sc[:, q * JP : (q + 1) * JP],
                    start=True,
                    stop=True,
                )
                if copy == 0:
                    a_scalar.append(bank)
            a_ps.append(bank)

        s1 = floats("s1")
        s2 = floats("s2")
        sq = [sb.tile([P, JH], F32, name="sq%d" % h, align_bytes=64) for h in range(HALVES)]
        per_half = PIECES // HALVES
        for q in range(PIECES):
            place = q % per_half
            nc.scalar.activation(sq[q // per_half][:, place * JP : (place + 1) * JP], a_scalar[q][:], ACT.Square)
        for h in range(HALVES):
            for q in range(h * per_half, (h + 1) * per_half):
                nc.vector.tensor_reduce(s1[:, q * GP : (q + 1) * GP], grouped(a_ps[q][:]), AX.X, add)
            nc.vector.tensor_reduce(s2[:, h * GH : (h + 1) * GH], grouped(sq[h][:]), AX.X, add)

        nq = floats("nq")
        nc.vector.scalar_tensor_tensor(nq[:], s1[:], -1.0 / POOL, s1[:], mult, mult)
        a_last = floats("a_last", JP)
        nc.scalar.copy(a_last[:], a_scalar[LAST][:])
        var8 = floats("var8")
        nc.vector.tensor_tensor(var8[:], s2[:], nq[:], add)
        y = floats("y")
        nc.scalar.activation(y[:], var8[:], ACT.Abs_reciprocal_sqrt, bias=EPS, scale=1.0 / POOL)

        s8 = floats("s8")
        nc.vector.scalar_tensor_tensor(s8[:], var8[:], POOL * EPS, y[:], add, mult)
        x8 = floats("x8")
        nc.vector.scalar_tensor_tensor(x8[:], s1[:], share_sb[:], s8[:], mult, add)
        u = floats("u")
        nc.scalar.activation(u[:], x8[:], ACT.Tanh, scale=1.0 / POOL)

        wo_codes, wo_scales = quantise("wo", wo_raw, R, nc.vector.tensor_copy, "word_win", "wo_codes")
        dy_codes, dy_scales = quantise("dy", dy_raw, G, nc.scalar.copy, "w1_codes", "sq1")
        c_ps = psum.tile([P, G], F32, name="c_ps")
        nc.tensor.matmul_mx(
            out=c_ps[:],
            lhsT=wo_codes[:].bitcast(FP8X4),
            lhsT_scale=wo_scales[:],
            rhs=dy_codes[:].bitcast(FP8X4),
            rhs_scale=dy_scales[:],
            start=True,
            stop=True,
        )
        h_top = floats("h_top", 1)
        nc.vector.tensor_scalar(h_top[:], share_sb[:], share_sb[:], 1.0, mult, add)
        cg = floats("cg")
        nc.vector.tensor_scalar(cg[:], c_ps[:], og_sb[:], 1.0 / (2 * POOL), mult, mult)
        cc = floats("cc")
        nc.vector.tensor_tensor(cc[:], c_ps[:], cg[:], mult)

        y2 = floats("y2")
        nc.vector.tensor_tensor(y2[:], y[:], y[:], mult)
        nmy = floats("nmy")
        nc.vector.scalar_tensor_tensor(nmy[:], s1[:], -1.0 / POOL, y[:], mult, mult)
        hh = floats("hh")
        nc.vector.tensor_scalar(hh[:], y2[:], -EPS, h_top[:], mult, add)
        fixed, slope = 0, 2
        raw_terms = sb.tile([P, 4, G], F32, name="raw_terms")
        nc.vector.scalar_tensor_tensor(raw_terms[:, fixed + GAIN, :], y2[:], EPS / 2, y2[:], mult, mult)
        nc.vector.tensor_tensor(raw_terms[:, slope + GAIN, :], hh[:], y[:], mult)
        nc.vector.scalar_tensor_tensor(raw_terms[:, slope + OFFSET, :], nmy[:], share_sb[:], hh[:], add, mult)
        nc.vector.scalar_tensor_tensor(raw_terms[:, fixed + OFFSET, :], s1[:], -1.0 / POOL, raw_terms[:, fixed + GAIN, :], mult, mult)
        terms = sb.tile([P, 4, G], F32, name="terms")
        for j in (slope, fixed):
            nc.vector.tensor_tensor(terms[:, j : j + 2, :], raw_terms[:, j : j + 2, :], cc[:].unsqueeze(1).to_broadcast([P, 2, G]), mult)

        u2 = floats("u2")
        nc.scalar.activation(u2[:], u[:], ACT.Square)
        w2 = floats("w2")
        nc.scalar.activation(w2[:], u2[:], ACT.Square, bias=1.0, scale=-1.0)
        us = sb.tile([P, 2, G], F32, name="us")
        inner = sb.tile([P, 2, G], F32, name="inner")
        coef = sb.tile([P, 2, G], F32, name="coef")
        for j in (OFFSET, GAIN):
            nc.vector.tensor_tensor(us[:, j, :], terms[:, slope + j, :], u[:], mult)
        for j in (OFFSET, GAIN):
            nc.vector.tensor_tensor(inner[:, j, :], terms[:, fixed + j, :], us[:, j, :], sub)
        for j in (OFFSET, GAIN):
            nc.vector.tensor_tensor(coef[:, j, :], inner[:, j, :], w2[:], mult)

        scaled = floats("scaled", J)
        for g in range(GP):
            group = LAST * GP + g
            nc.scalar.activation(
                scaled[:, group * POOL : (group + 1) * POOL],
                a_last[:, g * POOL : (g + 1) * POOL],
                ACT.Identity,
                bias=coef[:, OFFSET, group : group + 1],
                scale=coef[:, GAIN, group : group + 1],
            )
        res = floats("res", J)
        nc.vector.tensor_tensor(grouped(base_sb[:, 0:JV]), grouped(base_sb[:, 0:JV]), spread(coef[:, OFFSET, 0 : LAST * GP]), add)
        for q in range(LAST):
            nc.vector.tensor_tensor(
                grouped(scaled[:, q * JP : (q + 1) * JP]), grouped(a_ps[q][:]), spread(coef[:, GAIN, q * GP : (q + 1) * GP]), mult
            )
        for cols in (slice(0, JH), slice(JH, JV), slice(JV, J)):
            nc.vector.tensor_tensor(res[:, cols], scaled[:, cols], base_sb[:, cols], add)
            nc.sync.dma_start(out[:, cols], res[:, cols])
